import numpy as np
import ml_dtypes


def mxq(x, axis, fmt="e4m3"):
    dtype, down = {"e4m3": (ml_dtypes.float8_e4m3fn, 7), "e5m2": (ml_dtypes.float8_e5m2, 14)}[fmt]
    v = np.moveaxis(np.asarray(x, np.float32).astype(ml_dtypes.bfloat16).astype(np.float64), axis, -1)
    blocks = v.reshape(v.shape[:-1] + (-1, 32))
    amax = np.abs(blocks).max(-1, keepdims=True)
    byte = np.maximum(np.where(amax > 0, np.frexp(amax)[1] - 1 + 127, 0) - down, 1)
    scale = np.exp2(byte - 127.0)
    codes = (blocks / scale).astype(np.float32).astype(dtype).astype(np.float64)
    return np.moveaxis((codes * scale).reshape(v.shape), -1, axis)


WIDE = False


def mx_kscale(k):
    if not WIDE:
        return np.ones(k)
    levels = np.array([10, -10, 5, -5, 0])
    if k % 512:
        return np.exp2(np.random.permutation(np.resize(levels, k // 32))).repeat(32)
    a = np.empty((k // 512, 16))
    for p in range(k // 512):
        a[p, :8] = np.random.permutation(np.resize(levels, 8))
        for g in range(8):
            far = levels[np.abs(levels - a[p, g]) >= 10]
            a[p, g + 8] = far[np.random.randint(len(far))]
    return np.exp2(a.ravel()).repeat(32)


def f64(x):
    return np.asarray(x).astype(np.float64)


def striped(idx):
    return np.tile(idx.reshape(-1, 16).T, (8, 1)).astype(np.uint16)


def unstriped(offs):
    return offs[:16].T.reshape(-1).astype(np.int64)


def striped8(idx):
    return np.concatenate([x.reshape(-1, 16).T for x in idx]).astype(np.uint16)


def runs(offs, k):
    lists = np.stack([offs[16 * r : 16 * r + 16].T.reshape(-1) for r in range(8)]).astype(np.int64)
    return lists[np.arange(k) % 512 // 64]


def pack_weight(w):
    k, n = w.shape
    w = f64(np.asarray(w, np.float32).astype(ml_dtypes.bfloat16)).reshape(k // 32, 32, n)
    amax = np.abs(w).max(1)
    byte = np.clip(np.where(amax > 0, np.frexp(amax)[1] - 1 + 127 - 7, 1), 1, 254)
    scaled = (w * np.exp2(127.0 - byte)[:, None, :]).reshape(k, n).astype(np.float32)
    words = np.ascontiguousarray(scaled.reshape(k // 512, 128, 4, n).transpose(0, 1, 3, 2)).astype(ml_dtypes.float8_e4m3fn).view(np.uint8)
    return words, np.ascontiguousarray(byte.astype(np.uint8).reshape(k // 512, 16, n))


def unpack_weight(words, scales):
    g, p, n, _ = words.shape
    vals = np.ascontiguousarray(words).view(ml_dtypes.float8_e4m3fn).astype(np.float64) * np.repeat(np.exp2(scales.astype(np.float64) - 127.0), 8, axis=1)[..., None]
    return vals.transpose(0, 1, 3, 2).reshape(g * 512, n)


K, T, S, H, G, U = 512, 2048, 256, 512, 2048, 512


def setup_inputs():
    n = np.random.standard_normal
    s = mx_kscale(K)[:, None]
    packed_xT = pack_weight(n((K, T)) * s)
    packed_dT = pack_weight(n((K, G)) / s)
    perm = np.random.permutation(U)
    return {
        "x_words": packed_xT[0],
        "x_scales": packed_xT[1],
        "w1": (n((K, H)) / np.sqrt(K) / s).astype(np.float32),
        "gs": (np.random.uniform(0.5, 1.5, (K, 1)) * s).astype(np.float32),
        "d_words": packed_dT[0],
        "d_scales": packed_dT[1],
        "offs": striped(np.random.permutation(T)[:S]),
        "ka": striped8(np.random.randint(0, G, (8, H))),
        "kb": striped8(np.random.randint(0, G, (8, H))),
        "n1": striped(perm[:S]),
        "n2": striped(perm[S:]),
        "n3": striped(np.random.permutation(S)),
    }


def reference(x_words, x_scales, w1, gs, d_words, d_scales, offs, ka, kb, n1, n2, n3):
    d_ka = unpack_weight(d_words, d_scales)[np.arange(K)[:, None], runs(ka, K)]
    xq = unpack_weight(x_words, x_scales)[:, unstriped(offs)]
    y = mxq(f64(w1), 0, "e4m3").T @ xq
    z = f64(gs) * y
    zq = mxq(z, 0, "e4m3")
    d_kb = unpack_weight(d_words, d_scales)[np.arange(K)[:, None], runs(kb, K)]
    h = 0.0625 * (d_ka.T @ zq + d_kb.T @ zq)
    nw = h - h[:, unstriped(n3)]
    ph = np.zeros((H, U))
    ph[:, unstriped(n1)] = h
    out = ph.copy()
    out[:, unstriped(n2)] = nw
    return out

@@ -1,0 +1,163 @@
+from contextlib import ExitStack
+
+import concourse.mybir as mybir
+
+F32 = mybir.dt.float32
+BF16 = mybir.dt.bfloat16
+I32 = mybir.dt.int32
+U32 = mybir.dt.uint32
+U16 = mybir.dt.uint16
+U8 = mybir.dt.uint8
+FP8X4 = mybir.dt.float8_e4m3fn_x4
+COPY = mybir.ActivationFunctionType.Copy
+MULT = mybir.AluOpType.mult
+SUBTRACT = mybir.AluOpType.subtract
+
+P = 128
+PACK = 4
+K, T, S, H, G, U = 512, 2048, 256, 512, 2048, 512
+FLOPS = 2 * K * H * S * 3
+
+
+def tile_picked_daqipagq_none_p_kernel(
+    tc, x_words, x_scales, w1, gs, d_words, d_scales, offs, ka, kb, n1, n2, n3, out
+):
+    nc = tc.nc
+    with ExitStack() as ctx:
+        sb = ctx.enter_context(tc.tile_pool(name="sb", bufs=1))
+        psum = ctx.enter_context(tc.psum_pool(name="psum", bufs=1))
+
+        def load_list(name, dram):
+            tile = sb.tile(list(dram.shape), U16, name=name)
+            nc.sync.dma_start(tile[:], dram)
+            return tile
+
+        d_scale_table = sb.tile([P, G], U8)
+        nc.vector.memset(d_scale_table[:].bitcast(I32), 0)
+        x_scale_table = sb.tile([P, T], U8, tag="reused")
+        nc.gpsimd.memset(x_scale_table[:].bitcast(I32), 0)
+        early_planes = sb.tile([P, 3 * S], U8, align_bytes=64)
+        nc.vector.memset(early_planes[:].bitcast(I32), 0)
+        late_planes = sb.tile([P, 2 * S], U8, align_bytes=64)
+        nc.vector.memset(late_planes[:].bitcast(I32), 0)
+
+        ka_list = load_list("ka_list", ka)
+        kb_list = load_list("kb_list", kb)
+        offs_list = load_list("offs_list", offs)
+        nc.sync.dma_start(d_scale_table[0:P:8, :].bitcast(I32), d_scales[0].bitcast(I32))
+        nc.sync.dma_start(x_scale_table[0:P:8, :].bitcast(I32), x_scales[0].bitcast(I32))
+        w_raw = sb.tile([P, PACK, H], F32)
+        nc.sync.dma_start(w_raw[:], w1.rearrange("(p j) c -> p j c", j=PACK))
+        gains = sb.tile([P, PACK], F32)
+        nc.sync.dma_start(gains[:], gs.rearrange("(p t) o -> p (t o)", t=PACK))
+        n1_list = load_list("n1_list", n1)
+        x_table = sb.tile([P, T], U32)
+        nc.sync.dma_start(x_table[:].bitcast(I32), x_words[0].rearrange("p n r -> p (n r)").bitcast(I32))
+        n3_list = load_list("n3_list", n3)
+        n2_list = load_list("n2_list", n2)
+
+        def move_scale_rows(queue, planes, picked):
+            for q in range(4):
+                queue.dma_start(
+                    planes[32 * q : 32 * q + 4, :].bitcast(I32), picked[32 * q : 32 * q + 32 : 8, :].bitcast(I32)
+                )
+
+        early_picked = sb.tile([P, 3 * S], U8)
+        for c, codes in enumerate((ka_list, kb_list)):
+            nc.vector.tensor_copy(early_picked[:, c * S : (c + 1) * S], d_scale_table[:].indirect(codes[:, 0:16]))
+        nc.vector.tensor_copy(early_picked[:, 2 * S :], x_scale_table[:].indirect(offs_list[:]))
+        move_scale_rows(nc.sync, early_planes, early_picked)
+        d_table = sb.tile([P, G], U32, tag="reused")
+        nc.sync.dma_start(d_table[:].bitcast(I32), d_words[0].rearrange("p n r -> p (n r)").bitcast(I32))
+
+        w_codes = sb.tile([P, H], U32, align_bytes=64)
+        w_plane = sb.tile([P, H], U8, align_bytes=64)
+        half = P // 2
+        w_by_m = w_raw[:].rearrange("p j (m t) -> p m j t", t=PACK)
+        w_grouped = []
+        for u, copy in enumerate((nc.vector.tensor_copy, nc.scalar.copy)):
+            grouped = sb.tile([P, PACK, half, PACK], BF16, align_bytes=64, name=f"w_grouped{u}")
+            copy(grouped[:].rearrange("p t m j -> p m j t"), w_by_m[:, u * half : (u + 1) * half])
+            w_grouped.append(grouped)
+        for u in range(2):
+            for t in range(PACK):
+                cols = slice(t * P + u * half, t * P + (u + 1) * half)
+                nc.vector.quantize_mx(
+                    out=w_codes[:, cols].bitcast(FP8X4),
+                    scales=w_plane[:, cols],
+                    in_=w_grouped[u][:, t].rearrange("p m j -> p (m j)"),
+                )
+
+        z_codes = sb.tile([P, S], U32, align_bytes=64)
+        z_plane = sb.tile([P, S], U8, align_bytes=64)
+        x_picked = []
+        for u in range(2):
+            picked = sb.tile([P, P], U32, align_bytes=64, name=f"x_picked{u}")
+            nc.vector.tensor_copy(picked[:], x_table[:].indirect(offs_list[:, u * 8 : (u + 1) * 8]))
+            x_picked.append(picked)
+        z_rounded = []
+        for u in range(2):
+            y = psum.tile([P, PACK, P], F32, name=f"y{u}")
+            for t in range(PACK):
+                nc.tensor.matmul_mx(
+                    out=y[:, t, :],
+                    lhsT=w_codes[:, t * P : (t + 1) * P].bitcast(FP8X4),
+                    lhsT_scale=w_plane[:, t * P : (t + 1) * P],
+                    rhs=x_picked[u][:].bitcast(FP8X4),
+                    rhs_scale=early_planes[:, 2 * S + u * P : 2 * S + (u + 1) * P],
+                    start=True,
+                    stop=True,
+                )
+            rounded = sb.tile([P, P, PACK], BF16, align_bytes=64, name=f"z_rounded{u}")
+            nc.vector.tensor_tensor(
+                rounded[:], y[:].rearrange("p t n -> p n t"), gains[:].unsqueeze(1).to_broadcast([P, P, PACK]), MULT
+            )
+            z_rounded.append(rounded)
+        for u in range(2):
+            nc.vector.quantize_mx(
+                out=z_codes[:, u * P : (u + 1) * P].bitcast(FP8X4),
+                scales=z_plane[:, u * P : (u + 1) * P],
+                in_=z_rounded[u][:].rearrange("p n t -> p (n t)"),
+            )
+
+        for pair in range(2):
+            if pair == 1:
+                late_picked = sb.tile([P, 2 * S], U8, align_bytes=64, tag="picked00")
+                for c, codes in enumerate((ka_list, kb_list)):
+                    nc.vector.tensor_copy(
+                        late_picked[:, c * S : (c + 1) * S], d_scale_table[:].indirect(codes[:, 16:32])
+                    )
+                move_scale_rows(nc.sync, late_planes, late_picked)
+            d_picked = []
+            for c, codes in enumerate((ka_list, kb_list)):
+                picked = sb.tile([P, 2 * P], U32, align_bytes=64, name=f"d_picked{pair}{c}", tag=f"picked{pair}{c}")
+                nc.vector.tensor_copy(picked[:], d_table[:].indirect(codes[:, pair * 16 : (pair + 1) * 16]))
+                d_picked.append(picked)
+            for b in (2 * pair, 2 * pair + 1):
+                acc = psum.tile([P, S], F32, name=f"acc{b}")
+                for c in range(2):
+                    nc.tensor.matmul_mx(
+                        out=acc[:],
+                        lhsT=d_picked[c][:, (b % 2) * P : (b % 2 + 1) * P].bitcast(FP8X4),
+                        lhsT_scale=(early_planes, late_planes)[pair][:, c * S + (b % 2) * P : c * S + (b % 2 + 1) * P],
+                        rhs=z_codes[:].bitcast(FP8X4),
+                        rhs_scale=z_plane[:],
+                        start=(c == 0),
+                        stop=(c == 1),
+                    )
+                h = sb.tile([P, S], F32, name=f"h{b}")
+                if b == 0:
+                    nc.scalar.activation(h[:], acc[:], COPY, scale=0.0625)
+                else:
+                    nc.vector.tensor_scalar_mul(h[:], acc[:], 0.0625)
+                fetched = sb.tile([P, S], F32, name=f"fetched{b}")
+                for u in range(2):
+                    nc.scalar.activation(
+                        fetched[:, u * P : (u + 1) * P], h[:].indirect(n3_list[:, u * 8 : (u + 1) * 8]), COPY
+                    )
+                page = sb.tile([P, U], F32, name=f"page{b}")
+                nc.scalar.activation(page[:].indirect(n1_list[:]), h[:], COPY)
+                nw = sb.tile([P, S], F32, name=f"nw{b}")
+                nc.vector.tensor_tensor(nw[:], h[:], fetched[:], SUBTRACT)
+                nc.scalar.activation(page[:].indirect(n2_list[:]), nw[:], COPY)
+                (nc.sync if b >= 2 else nc.gpsimd).dma_start(out[b * P : (b + 1) * P, :], page[:])

@@ -16,6 +16,7 @@ SUBTRACT = mybir.AluOpType.subtract
 P = 128
 PACK = 4
 K, T, S, H, G, U = 512, 2048, 256, 512, 2048, 512
+SPARE = 16
 FLOPS = 2 * K * H * S * 3
 
 
@@ -34,62 +35,62 @@ def tile_picked_daqipagq_none_p_kernel(
 
         d_scale_table = sb.tile([P, G], U8)
         nc.vector.memset(d_scale_table[:].bitcast(I32), 0)
-        x_scale_table = sb.tile([P, T], U8, tag="reused")
+        x_scale_table = sb.tile([P, T], U8)
         nc.gpsimd.memset(x_scale_table[:].bitcast(I32), 0)
-        early_planes = sb.tile([P, 3 * S], U8, align_bytes=64)
-        nc.vector.memset(early_planes[:].bitcast(I32), 0)
-        late_planes = sb.tile([P, 2 * S], U8, align_bytes=64)
-        nc.vector.memset(late_planes[:].bitcast(I32), 0)
+        d_planes = sb.tile([P, 2 * H], U8, align_bytes=64)
+        nc.vector.memset(d_planes[:].bitcast(I32), 0)
+        h = [sb.tile([P, S + SPARE], F32, name=f"h{b}") for b in range(4)]
+        for b in range(4):
+            nc.vector.memset(h[b][:, S:], 0.0)
 
         ka_list = load_list("ka_list", ka)
         kb_list = load_list("kb_list", kb)
         offs_list = load_list("offs_list", offs)
         nc.sync.dma_start(d_scale_table[0:P:8, :].bitcast(I32), d_scales[0].bitcast(I32))
-        nc.sync.dma_start(x_scale_table[0:P:8, :].bitcast(I32), x_scales[0].bitcast(I32))
         w_raw = sb.tile([P, PACK, H], F32)
         nc.sync.dma_start(w_raw[:], w1.rearrange("(p j) c -> p j c", j=PACK))
+        for q in range(4):
+            nc.sync.dma_start(
+                x_scale_table[32 * q : 32 * q + 4, :].bitcast(I32), x_scales[0, 4 * q : 4 * q + 4, :].bitcast(I32)
+            )
         gains = sb.tile([P, PACK], F32)
         nc.sync.dma_start(gains[:], gs.rearrange("(p t) o -> p (t o)", t=PACK))
-        n1_list = load_list("n1_list", n1)
         x_table = sb.tile([P, T], U32)
         nc.sync.dma_start(x_table[:].bitcast(I32), x_words[0].rearrange("p n r -> p (n r)").bitcast(I32))
+        d_table = sb.tile([P, G], U32)
+        nc.sync.dma_start(d_table[:].bitcast(I32), d_words[0].rearrange("p n r -> p (n r)").bitcast(I32))
+        n1_list = load_list("n1_list", n1)
         n3_list = load_list("n3_list", n3)
         n2_list = load_list("n2_list", n2)
 
-        def move_scale_rows(queue, planes, picked):
-            for q in range(4):
-                queue.dma_start(
-                    planes[32 * q : 32 * q + 4, :].bitcast(I32), picked[32 * q : 32 * q + 32 : 8, :].bitcast(I32)
-                )
-
-        early_picked = sb.tile([P, 3 * S], U8)
+        d_scales_picked = sb.tile([P, 2 * H], U8)
         for c, codes in enumerate((ka_list, kb_list)):
-            nc.vector.tensor_copy(early_picked[:, c * S : (c + 1) * S], d_scale_table[:].indirect(codes[:, 0:16]))
-        nc.vector.tensor_copy(early_picked[:, 2 * S :], x_scale_table[:].indirect(offs_list[:]))
-        move_scale_rows(nc.sync, early_planes, early_picked)
-        d_table = sb.tile([P, G], U32, tag="reused")
-        nc.sync.dma_start(d_table[:].bitcast(I32), d_words[0].rearrange("p n r -> p (n r)").bitcast(I32))
+            nc.vector.tensor_copy(d_scales_picked[:, c * H : (c + 1) * H], d_scale_table[:].indirect(codes[:]))
+        for q in range(4):
+            nc.sync.dma_start(
+                d_planes[32 * q : 32 * q + 4, :].bitcast(I32), d_scales_picked[32 * q : 32 * q + 32 : 8, :].bitcast(I32)
+            )
 
         w_codes = sb.tile([P, H], U32, align_bytes=64)
         w_plane = sb.tile([P, H], U8, align_bytes=64)
-        half = P // 2
         w_by_m = w_raw[:].rearrange("p j (m t) -> p m j t", t=PACK)
         w_grouped = []
         for u, copy in enumerate((nc.vector.tensor_copy, nc.scalar.copy)):
-            grouped = sb.tile([P, PACK, half, PACK], BF16, align_bytes=64, name=f"w_grouped{u}")
-            copy(grouped[:].rearrange("p t m j -> p m j t"), w_by_m[:, u * half : (u + 1) * half])
+            grouped = sb.tile([P, 2, P, PACK], BF16, align_bytes=64, name=f"w_grouped{u}")
+            copy(grouped[:].rearrange("p t m j -> p m j t"), w_by_m[:, :, :, 2 * u : 2 * u + 2])
             w_grouped.append(grouped)
+        x_plane = sb.tile([P, S], U8, align_bytes=64)
+        nc.vector.tensor_copy(x_plane[:], x_scale_table[:].indirect(offs_list[:]))
         for u in range(2):
-            for t in range(PACK):
-                cols = slice(t * P + u * half, t * P + (u + 1) * half)
-                nc.vector.quantize_mx(
-                    out=w_codes[:, cols].bitcast(FP8X4),
-                    scales=w_plane[:, cols],
-                    in_=w_grouped[u][:, t].rearrange("p m j -> p (m j)"),
-                )
+            cols = slice(2 * u * P, 2 * (u + 1) * P)
+            nc.vector.quantize_mx(
+                out=w_codes[:, cols].bitcast(FP8X4),
+                scales=w_plane[:, cols],
+                in_=w_grouped[u][:].rearrange("p t m j -> p (t m j)"),
+            )
 
         z_codes = sb.tile([P, S], U32, align_bytes=64)
-        z_plane = sb.tile([P, S], U8, align_bytes=64)
+        z_planes = sb.tile([P, P], U8, align_bytes=64)
         x_picked = []
         for u in range(2):
             picked = sb.tile([P, P], U32, align_bytes=64, name=f"x_picked{u}")
@@ -104,60 +105,69 @@ def tile_picked_daqipagq_none_p_kernel(
                     lhsT=w_codes[:, t * P : (t + 1) * P].bitcast(FP8X4),
                     lhsT_scale=w_plane[:, t * P : (t + 1) * P],
                     rhs=x_picked[u][:].bitcast(FP8X4),
-                    rhs_scale=early_planes[:, 2 * S + u * P : 2 * S + (u + 1) * P],
+                    rhs_scale=x_plane[:, u * P : (u + 1) * P],
                     start=True,
                     stop=True,
                 )
             rounded = sb.tile([P, P, PACK], BF16, align_bytes=64, name=f"z_rounded{u}")
-            nc.vector.tensor_tensor(
-                rounded[:], y[:].rearrange("p t n -> p n t"), gains[:].unsqueeze(1).to_broadcast([P, P, PACK]), MULT
-            )
+            if u == 0:
+                nc.vector.tensor_tensor(
+                    rounded[:], y[:].rearrange("p t n -> p n t"), gains[:].unsqueeze(1).to_broadcast([P, P, PACK]), MULT
+                )
+            else:
+                for t in range(PACK):
+                    nc.scalar.activation(rounded[:, :, t], y[:, t, :], COPY, scale=gains[:, t : t + 1])
             z_rounded.append(rounded)
-        for u in range(2):
+
+        def quantize_z(u):
             nc.vector.quantize_mx(
                 out=z_codes[:, u * P : (u + 1) * P].bitcast(FP8X4),
-                scales=z_plane[:, u * P : (u + 1) * P],
+                scales=z_planes[4 * u :, :],
                 in_=z_rounded[u][:].rearrange("p n t -> p (n t)"),
             )
 
+        quantize_z(0)
+
+        def second_product(acc, b, d_picked, u):
+            for c in range(2):
+                nc.tensor.matmul_mx(
+                    out=acc,
+                    lhsT=d_picked[c][:, (b % 2) * P : (b % 2 + 1) * P].bitcast(FP8X4),
+                    lhsT_scale=d_planes[:, c * H + b * P : c * H + (b + 1) * P],
+                    rhs=z_codes[:, u * P : (u + 1) * P].bitcast(FP8X4),
+                    rhs_scale=z_planes[4 * u :, :],
+                    start=(c == 0),
+                    stop=(c == 1),
+                )
+
         for pair in range(2):
-            if pair == 1:
-                late_picked = sb.tile([P, 2 * S], U8, align_bytes=64, tag="picked00")
-                for c, codes in enumerate((ka_list, kb_list)):
-                    nc.vector.tensor_copy(
-                        late_picked[:, c * S : (c + 1) * S], d_scale_table[:].indirect(codes[:, 16:32])
-                    )
-                move_scale_rows(nc.sync, late_planes, late_picked)
             d_picked = []
             for c, codes in enumerate((ka_list, kb_list)):
-                picked = sb.tile([P, 2 * P], U32, align_bytes=64, name=f"d_picked{pair}{c}", tag=f"picked{pair}{c}")
+                picked = sb.tile([P, 2 * P], U32, align_bytes=64, name=f"d_picked{pair}{c}", tag=f"d_picked{c}")
                 nc.vector.tensor_copy(picked[:], d_table[:].indirect(codes[:, pair * 16 : (pair + 1) * 16]))
                 d_picked.append(picked)
             for b in (2 * pair, 2 * pair + 1):
-                acc = psum.tile([P, S], F32, name=f"acc{b}")
-                for c in range(2):
-                    nc.tensor.matmul_mx(
-                        out=acc[:],
-                        lhsT=d_picked[c][:, (b % 2) * P : (b % 2 + 1) * P].bitcast(FP8X4),
-                        lhsT_scale=(early_planes, late_planes)[pair][:, c * S + (b % 2) * P : c * S + (b % 2 + 1) * P],
-                        rhs=z_codes[:].bitcast(FP8X4),
-                        rhs_scale=z_plane[:],
-                        start=(c == 0),
-                        stop=(c == 1),
-                    )
-                h = sb.tile([P, S], F32, name=f"h{b}")
-                if b == 0:
-                    nc.scalar.activation(h[:], acc[:], COPY, scale=0.0625)
-                else:
-                    nc.vector.tensor_scalar_mul(h[:], acc[:], 0.0625)
-                fetched = sb.tile([P, S], F32, name=f"fetched{b}")
-                for u in range(2):
-                    nc.scalar.activation(
-                        fetched[:, u * P : (u + 1) * P], h[:].indirect(n3_list[:, u * 8 : (u + 1) * 8]), COPY
-                    )
                 page = sb.tile([P, U], F32, name=f"page{b}")
-                nc.scalar.activation(page[:].indirect(n1_list[:]), h[:], COPY)
+                fetched = sb.tile([P, S], F32, name=f"fetched{b}")
+                if b == 0:
+                    acc = psum.tile([P, P], F32, name="acc_first")
+                    second_product(acc[:], b, d_picked, 0)
+                    nc.scalar.activation(h[b][:, 0:P], acc[:], COPY, scale=0.0625)
+                    nc.scalar.activation(page[:].indirect(n1_list[:, 0:8]), h[b][:, 0:P], COPY)
+                    quantize_z(1)
+                    acc = psum.tile([P, P], F32, name="acc0")
+                    second_product(acc[:], b, d_picked, 1)
+                    nc.vector.tensor_scalar_mul(h[b][:, P:S], acc[:], 0.0625)
+                    nc.scalar.activation(fetched[:], h[b][:].indirect(n3_list[:]), COPY)
+                    nc.scalar.activation(page[:].indirect(n1_list[:, 8:16]), h[b][:, P:S], COPY)
+                else:
+                    acc = psum.tile([P, S], F32, name=f"acc{b}")
+                    for u in range(2):
+                        second_product(acc[:, u * P : (u + 1) * P], b, d_picked, u)
+                    nc.vector.tensor_scalar_mul(h[b][:, 0:S], acc[:], 0.0625)
+                    nc.scalar.activation(fetched[:], h[b][:].indirect(n3_list[:]), COPY)
+                    nc.scalar.activation(page[:].indirect(n1_list[:]), h[b][:, 0:S], COPY)
                 nw = sb.tile([P, S], F32, name=f"nw{b}")
-                nc.vector.tensor_tensor(nw[:], h[:], fetched[:], SUBTRACT)
+                nc.vector.tensor_tensor(nw[:], h[b][:, 0:S], fetched[:], SUBTRACT)
                 nc.scalar.activation(page[:].indirect(n2_list[:]), nw[:], COPY)
-                (nc.sync if b >= 2 else nc.gpsimd).dma_start(out[b * P : (b + 1) * P, :], page[:])
+                nc.sync.dma_start(out[b * P : (b + 1) * P, :], page[:])

@@ -35,10 +35,12 @@ def tile_picked_daqipagq_none_p_kernel(
 
         d_scale_table = sb.tile([P, G], U8)
         nc.vector.memset(d_scale_table[:].bitcast(I32), 0)
-        x_scale_table = sb.tile([P, T], U8)
-        nc.gpsimd.memset(x_scale_table[:].bitcast(I32), 0)
-        d_planes = sb.tile([P, 2 * H], U8, align_bytes=64)
-        nc.vector.memset(d_planes[:].bitcast(I32), 0)
+        x_scale_table = sb.tile([P, T], U8, tag="x_scales_then_d_words")
+        nc.vector.memset(x_scale_table[:].bitcast(I32), 0)
+        early_planes = sb.tile([P, 3 * S], U8, align_bytes=64)
+        nc.vector.memset(early_planes[:].bitcast(I32), 0)
+        late_planes = sb.tile([P, 2 * S], U8, align_bytes=64)
+        nc.vector.memset(late_planes[:].bitcast(I32), 0)
         h = [sb.tile([P, S + SPARE], F32, name=f"h{b}") for b in range(4)]
         for b in range(4):
             nc.vector.memset(h[b][:, S:], 0.0)
@@ -47,29 +49,30 @@ def tile_picked_daqipagq_none_p_kernel(
         kb_list = load_list("kb_list", kb)
         offs_list = load_list("offs_list", offs)
         nc.sync.dma_start(d_scale_table[0:P:8, :].bitcast(I32), d_scales[0].bitcast(I32))
-        w_raw = sb.tile([P, PACK, H], F32)
-        nc.sync.dma_start(w_raw[:], w1.rearrange("(p j) c -> p j c", j=PACK))
-        for q in range(4):
-            nc.sync.dma_start(
-                x_scale_table[32 * q : 32 * q + 4, :].bitcast(I32), x_scales[0, 4 * q : 4 * q + 4, :].bitcast(I32)
-            )
         gains = sb.tile([P, PACK], F32)
         nc.sync.dma_start(gains[:], gs.rearrange("(p t) o -> p (t o)", t=PACK))
+        nc.sync.dma_start(x_scale_table[0:P:8, :].bitcast(I32), x_scales[0].bitcast(I32))
+        w_raw = sb.tile([P, PACK, H], F32)
+        nc.sync.dma_start(w_raw[:], w1.rearrange("(p j) c -> p j c", j=PACK))
+        n1_list = load_list("n1_list", n1)
         x_table = sb.tile([P, T], U32)
         nc.sync.dma_start(x_table[:].bitcast(I32), x_words[0].rearrange("p n r -> p (n r)").bitcast(I32))
-        d_table = sb.tile([P, G], U32)
-        nc.sync.dma_start(d_table[:].bitcast(I32), d_words[0].rearrange("p n r -> p (n r)").bitcast(I32))
-        n1_list = load_list("n1_list", n1)
         n3_list = load_list("n3_list", n3)
         n2_list = load_list("n2_list", n2)
 
-        d_scales_picked = sb.tile([P, 2 * H], U8)
+        def move_scale_rows(planes, picked):
+            for q in range(4):
+                nc.sync.dma_start(
+                    planes[32 * q : 32 * q + 4, :].bitcast(I32), picked[32 * q : 32 * q + 32 : 8, :].bitcast(I32)
+                )
+
+        early_picked = sb.tile([P, 3 * S], U8)
         for c, codes in enumerate((ka_list, kb_list)):
-            nc.vector.tensor_copy(d_scales_picked[:, c * H : (c + 1) * H], d_scale_table[:].indirect(codes[:]))
-        for q in range(4):
-            nc.sync.dma_start(
-                d_planes[32 * q : 32 * q + 4, :].bitcast(I32), d_scales_picked[32 * q : 32 * q + 32 : 8, :].bitcast(I32)
-            )
+            nc.vector.tensor_copy(early_picked[:, c * S : (c + 1) * S], d_scale_table[:].indirect(codes[:, 0:16]))
+        nc.vector.tensor_copy(early_picked[:, 2 * S :], x_scale_table[:].indirect(offs_list[:]))
+        move_scale_rows(early_planes, early_picked)
+        d_table = sb.tile([P, G], U32, tag="x_scales_then_d_words")
+        nc.sync.dma_start(d_table[:].bitcast(I32), d_words[0].rearrange("p n r -> p (n r)").bitcast(I32))
 
         w_codes = sb.tile([P, H], U32, align_bytes=64)
         w_plane = sb.tile([P, H], U8, align_bytes=64)
@@ -79,8 +82,6 @@ def tile_picked_daqipagq_none_p_kernel(
             grouped = sb.tile([P, 2, P, PACK], BF16, align_bytes=64, name=f"w_grouped{u}")
             copy(grouped[:].rearrange("p t m j -> p m j t"), w_by_m[:, :, :, 2 * u : 2 * u + 2])
             w_grouped.append(grouped)
-        x_plane = sb.tile([P, S], U8, align_bytes=64)
-        nc.vector.tensor_copy(x_plane[:], x_scale_table[:].indirect(offs_list[:]))
         for u in range(2):
             cols = slice(2 * u * P, 2 * (u + 1) * P)
             nc.vector.quantize_mx(
@@ -105,7 +106,7 @@ def tile_picked_daqipagq_none_p_kernel(
                     lhsT=w_codes[:, t * P : (t + 1) * P].bitcast(FP8X4),
                     lhsT_scale=w_plane[:, t * P : (t + 1) * P],
                     rhs=x_picked[u][:].bitcast(FP8X4),
-                    rhs_scale=x_plane[:, u * P : (u + 1) * P],
+                    rhs_scale=early_planes[:, 2 * S + u * P : 2 * S + (u + 1) * P],
                     start=True,
                     stop=True,
                 )
@@ -133,7 +134,7 @@ def tile_picked_daqipagq_none_p_kernel(
                 nc.tensor.matmul_mx(
                     out=acc,
                     lhsT=d_picked[c][:, (b % 2) * P : (b % 2 + 1) * P].bitcast(FP8X4),
-                    lhsT_scale=d_planes[:, c * H + b * P : c * H + (b + 1) * P],
+                    lhsT_scale=(early_planes, late_planes)[b // 2][:, c * S + (b % 2) * P : c * S + (b % 2 + 1) * P],
                     rhs=z_codes[:, u * P : (u + 1) * P].bitcast(FP8X4),
                     rhs_scale=z_planes[4 * u :, :],
                     start=(c == 0),
@@ -141,11 +142,19 @@ def tile_picked_daqipagq_none_p_kernel(
                 )
 
         for pair in range(2):
-            d_picked = []
+            if pair == 0:
+                d_picked = [sb.tile([P, S], U32, align_bytes=64, name=f"d_picked{c}", tag=f"picked{c}")[:] for c in range(2)]
+            else:
+                late_picked = sb.tile([P, 2 * S], U8, align_bytes=64, tag="picked0")
+                for c, codes in enumerate((ka_list, kb_list)):
+                    nc.vector.tensor_copy(
+                        late_picked[:, c * S : (c + 1) * S], d_scale_table[:].indirect(codes[:, 16:32])
+                    )
+                move_scale_rows(late_planes, late_picked)
+                late_words = sb.tile([P, 2 * S], U32, align_bytes=64, tag="picked1")
+                d_picked = [late_words[:, c * S : (c + 1) * S] for c in range(2)]
             for c, codes in enumerate((ka_list, kb_list)):
-                picked = sb.tile([P, 2 * P], U32, align_bytes=64, name=f"d_picked{pair}{c}", tag=f"d_picked{c}")
-                nc.vector.tensor_copy(picked[:], d_table[:].indirect(codes[:, pair * 16 : (pair + 1) * 16]))
-                d_picked.append(picked)
+                nc.vector.tensor_copy(d_picked[c], d_table[:].indirect(codes[:, pair * 16 : (pair + 1) * 16]))
             for b in (2 * pair, 2 * pair + 1):
                 page = sb.tile([P, U], F32, name=f"page{b}")
                 fetched = sb.tile([P, S], F32, name=f"fetched{b}")
@@ -170,4 +179,4 @@ def tile_picked_daqipagq_none_p_kernel(
                 nw = sb.tile([P, S], F32, name=f"nw{b}")
                 nc.vector.tensor_tensor(nw[:], h[b][:, 0:S], fetched[:], SUBTRACT)
                 nc.scalar.activation(page[:].indirect(n2_list[:]), nw[:], COPY)
-                nc.sync.dma_start(out[b * P : (b + 1) * P, :], page[:])
+                (nc.sync if b >= 2 else nc.gpsimd).dma_start(out[b * P : (b + 1) * P, :], page[:])

@@ -112,22 +112,27 @@ def tile_picked_daqipagq_none_p_kernel(
                 )
             rounded = sb.tile([P, P, PACK], BF16, align_bytes=64, name=f"z_rounded{u}")
             if u == 0:
-                nc.vector.tensor_tensor(
-                    rounded[:], y[:].rearrange("p t n -> p n t"), gains[:].unsqueeze(1).to_broadcast([P, P, PACK]), MULT
-                )
+                for n0 in (0, P // 2):
+                    nc.vector.tensor_tensor(
+                        rounded[:, n0 : n0 + P // 2],
+                        y[:, :, n0 : n0 + P // 2].rearrange("p t n -> p n t"),
+                        gains[:].unsqueeze(1).to_broadcast([P, P // 2, PACK]),
+                        MULT,
+                    )
             else:
                 for t in range(PACK):
                     nc.scalar.activation(rounded[:, :, t], y[:, t, :], COPY, scale=gains[:, t : t + 1])
             z_rounded.append(rounded)
 
-        def quantize_z(u):
+        def quantize_z(u, n0, n1):
             nc.vector.quantize_mx(
-                out=z_codes[:, u * P : (u + 1) * P].bitcast(FP8X4),
-                scales=z_planes[4 * u :, :],
-                in_=z_rounded[u][:].rearrange("p n t -> p (n t)"),
+                out=z_codes[:, u * P + n0 : u * P + n1].bitcast(FP8X4),
+                scales=z_planes[4 * u :, n0:n1],
+                in_=z_rounded[u][:, n0:n1].rearrange("p n t -> p (n t)"),
             )
 
-        quantize_z(0)
+        quantize_z(0, 0, P // 2)
+        quantize_z(0, P // 2, P)
 
         def second_product(acc, b, d_picked, u):
             for c in range(2):
@@ -155,16 +160,23 @@ def tile_picked_daqipagq_none_p_kernel(
                 d_picked = [late_words[:, c * S : (c + 1) * S] for c in range(2)]
             for c, codes in enumerate((ka_list, kb_list)):
                 nc.vector.tensor_copy(d_picked[c], d_table[:].indirect(codes[:, pair * 16 : (pair + 1) * 16]))
-            for b in (2 * pair, 2 * pair + 1):
-                page = sb.tile([P, U], F32, name=f"page{b}")
-                fetched = sb.tile([P, S], F32, name=f"fetched{b}")
-                if b == 0:
-                    acc = psum.tile([P, P], F32, name="acc_first")
+            blocks = (2 * pair, 2 * pair + 1)
+            pages = {b: sb.tile([P, U], F32, name=f"page{b}") for b in blocks}
+            if pair == 0:
+                for b in blocks:
+                    acc = psum.tile([P, P], F32, name=f"acc_first{b}")
                     second_product(acc[:], b, d_picked, 0)
-                    nc.scalar.activation(h[b][:, 0:P], acc[:], COPY, scale=0.0625)
-                    nc.scalar.activation(page[:].indirect(n1_list[:, 0:8]), h[b][:, 0:P], COPY)
-                    quantize_z(1)
-                    acc = psum.tile([P, P], F32, name="acc0")
+                    if b == 0:
+                        nc.scalar.activation(h[b][:, 0:P], acc[:], COPY, scale=0.0625)
+                    else:
+                        nc.vector.tensor_scalar_mul(h[b][:, 0:P], acc[:], 0.0625)
+                    nc.scalar.activation(pages[b][:].indirect(n1_list[:, 0:8]), h[b][:, 0:P], COPY)
+                quantize_z(1, 0, P)
+            for b in blocks:
+                page = pages[b]
+                fetched = sb.tile([P, S], F32, name=f"fetched{b}")
+                if pair == 0:
+                    acc = psum.tile([P, P], F32, name=f"acc{b}")
                     second_product(acc[:], b, d_picked, 1)
                     nc.vector.tensor_scalar_mul(h[b][:, P:S], acc[:], 0.0625)
                     nc.scalar.activation(fetched[:], h[b][:].indirect(n3_list[:]), COPY)

from contextlib import ExitStack

import concourse.mybir as mybir

F32 = mybir.dt.float32
BF16 = mybir.dt.bfloat16
I32 = mybir.dt.int32
U32 = mybir.dt.uint32
U16 = mybir.dt.uint16
U8 = mybir.dt.uint8
FP8X4 = mybir.dt.float8_e4m3fn_x4
COPY = mybir.ActivationFunctionType.Copy
MULT = mybir.AluOpType.mult
SUBTRACT = mybir.AluOpType.subtract

P = 128
PACK = 4
K, T, S, H, G, U = 512, 2048, 256, 512, 2048, 512
SPARE = 16
FLOPS = 2 * K * H * S * 3


def tile_picked_daqipagq_none_p_kernel(
    tc, x_words, x_scales, w1, gs, d_words, d_scales, offs, ka, kb, n1, n2, n3, out
):
    nc = tc.nc
    with ExitStack() as ctx:
        sb = ctx.enter_context(tc.tile_pool(name="sb", bufs=1))
        psum = ctx.enter_context(tc.psum_pool(name="psum", bufs=1))

        def load_list(name, dram):
            tile = sb.tile(list(dram.shape), U16, name=name)
            nc.sync.dma_start(tile[:], dram)
            return tile

        d_scale_table = sb.tile([P, G], U8)
        nc.vector.memset(d_scale_table[:].bitcast(I32), 0)
        x_scale_table = sb.tile([P, T], U8, tag="x_scales_then_d_words")
        nc.vector.memset(x_scale_table[:].bitcast(I32), 0)
        early_planes = sb.tile([P, 3 * S], U8, align_bytes=64)
        nc.vector.memset(early_planes[:].bitcast(I32), 0)
        late_planes = sb.tile([P, 2 * S], U8, align_bytes=64)
        nc.vector.memset(late_planes[:].bitcast(I32), 0)
        h = [sb.tile([P, S + SPARE], F32, name=f"h{b}") for b in range(4)]
        for b in range(4):
            nc.vector.memset(h[b][:, S:], 0.0)

        ka_list = load_list("ka_list", ka)
        kb_list = load_list("kb_list", kb)
        offs_list = load_list("offs_list", offs)
        nc.sync.dma_start(d_scale_table[0:P:8, :].bitcast(I32), d_scales[0].bitcast(I32))
        gains = sb.tile([P, PACK], F32)
        nc.sync.dma_start(gains[:], gs.rearrange("(p t) o -> p (t o)", t=PACK))
        nc.sync.dma_start(x_scale_table[0:P:8, :].bitcast(I32), x_scales[0].bitcast(I32))
        w_raw = sb.tile([P, PACK, H], F32)
        nc.sync.dma_start(w_raw[:], w1.rearrange("(p j) c -> p j c", j=PACK))
        n1_list = load_list("n1_list", n1)
        x_table = sb.tile([P, T], U32)
        nc.sync.dma_start(x_table[:].bitcast(I32), x_words[0].rearrange("p n r -> p (n r)").bitcast(I32))
        n3_list = load_list("n3_list", n3)
        n2_list = load_list("n2_list", n2)

        def move_scale_rows(planes, picked):
            for q in range(4):
                nc.sync.dma_start(
                    planes[32 * q : 32 * q + 4, :].bitcast(I32), picked[32 * q : 32 * q + 32 : 8, :].bitcast(I32)
                )

        early_picked = sb.tile([P, 3 * S], U8)
        for c, codes in enumerate((ka_list, kb_list)):
            nc.vector.tensor_copy(early_picked[:, c * S : (c + 1) * S], d_scale_table[:].indirect(codes[:, 0:16]))
        nc.vector.tensor_copy(early_picked[:, 2 * S :], x_scale_table[:].indirect(offs_list[:]))
        move_scale_rows(early_planes, early_picked)
        d_table = sb.tile([P, G], U32, tag="x_scales_then_d_words")
        nc.sync.dma_start(d_table[:].bitcast(I32), d_words[0].rearrange("p n r -> p (n r)").bitcast(I32))

        w_codes = sb.tile([P, H], U32, align_bytes=64)
        w_plane = sb.tile([P, H], U8, align_bytes=64)
        w_by_m = w_raw[:].rearrange("p j (m t) -> p m j t", t=PACK)
        w_grouped = []
        for u, copy in enumerate((nc.vector.tensor_copy, nc.scalar.copy)):
            grouped = sb.tile([P, 2, P, PACK], BF16, align_bytes=64, name=f"w_grouped{u}")
            copy(grouped[:].rearrange("p t m j -> p m j t"), w_by_m[:, :, :, 2 * u : 2 * u + 2])
            w_grouped.append(grouped)
        for u in range(2):
            cols = slice(2 * u * P, 2 * (u + 1) * P)
            nc.vector.quantize_mx(
                out=w_codes[:, cols].bitcast(FP8X4),
                scales=w_plane[:, cols],
                in_=w_grouped[u][:].rearrange("p t m j -> p (t m j)"),
            )

        z_codes = sb.tile([P, S], U32, align_bytes=64)
        z_planes = sb.tile([P, P], U8, align_bytes=64)
        x_picked = []
        for u in range(2):
            picked = sb.tile([P, P], U32, align_bytes=64, name=f"x_picked{u}")
            nc.vector.tensor_copy(picked[:], x_table[:].indirect(offs_list[:, u * 8 : (u + 1) * 8]))
            x_picked.append(picked)
        z_rounded = []
        for u in range(2):
            y = psum.tile([P, PACK, P], F32, name=f"y{u}")
            for t in range(PACK):
                nc.tensor.matmul_mx(
                    out=y[:, t, :],
                    lhsT=w_codes[:, t * P : (t + 1) * P].bitcast(FP8X4),
                    lhsT_scale=w_plane[:, t * P : (t + 1) * P],
                    rhs=x_picked[u][:].bitcast(FP8X4),
                    rhs_scale=early_planes[:, 2 * S + u * P : 2 * S + (u + 1) * P],
                    start=True,
                    stop=True,
                )
            rounded = sb.tile([P, P, PACK], BF16, align_bytes=64, name=f"z_rounded{u}")
            if u == 0:
                for n0 in (0, P // 2):
                    nc.vector.tensor_tensor(
                        rounded[:, n0 : n0 + P // 2],
                        y[:, :, n0 : n0 + P // 2].rearrange("p t n -> p n t"),
                        gains[:].unsqueeze(1).to_broadcast([P, P // 2, PACK]),
                        MULT,
                    )
            else:
                for t in range(PACK):
                    nc.scalar.activation(rounded[:, :, t], y[:, t, :], COPY, scale=gains[:, t : t + 1])
            z_rounded.append(rounded)

        def quantize_z(u, n0, n1):
            nc.vector.quantize_mx(
                out=z_codes[:, u * P + n0 : u * P + n1].bitcast(FP8X4),
                scales=z_planes[4 * u :, n0:n1],
                in_=z_rounded[u][:, n0:n1].rearrange("p n t -> p (n t)"),
            )

        quantize_z(0, 0, P // 2)
        quantize_z(0, P // 2, P)

        def second_product(acc, b, d_picked, u):
            for c in range(2):
                nc.tensor.matmul_mx(
                    out=acc,
                    lhsT=d_picked[c][:, (b % 2) * P : (b % 2 + 1) * P].bitcast(FP8X4),
                    lhsT_scale=(early_planes, late_planes)[b // 2][:, c * S + (b % 2) * P : c * S + (b % 2 + 1) * P],
                    rhs=z_codes[:, u * P : (u + 1) * P].bitcast(FP8X4),
                    rhs_scale=z_planes[4 * u :, :],
                    start=(c == 0),
                    stop=(c == 1),
                )

        for pair in range(2):
            if pair == 0:
                d_picked = [sb.tile([P, S], U32, align_bytes=64, name=f"d_picked{c}", tag=f"picked{c}")[:] for c in range(2)]
            else:
                late_picked = sb.tile([P, 2 * S], U8, align_bytes=64, tag="picked0")
                for c, codes in enumerate((ka_list, kb_list)):
                    nc.vector.tensor_copy(
                        late_picked[:, c * S : (c + 1) * S], d_scale_table[:].indirect(codes[:, 16:32])
                    )
                move_scale_rows(late_planes, late_picked)
                late_words = sb.tile([P, 2 * S], U32, align_bytes=64, tag="picked1")
                d_picked = [late_words[:, c * S : (c + 1) * S] for c in range(2)]
            for c, codes in enumerate((ka_list, kb_list)):
                nc.vector.tensor_copy(d_picked[c], d_table[:].indirect(codes[:, pair * 16 : (pair + 1) * 16]))
            blocks = (2 * pair, 2 * pair + 1)
            pages = {b: sb.tile([P, U], F32, name=f"page{b}") for b in blocks}
            if pair == 0:
                for b in blocks:
                    acc = psum.tile([P, P], F32, name=f"acc_first{b}")
                    second_product(acc[:], b, d_picked, 0)
                    if b == 0:
                        nc.scalar.activation(h[b][:, 0:P], acc[:], COPY, scale=0.0625)
                    else:
                        nc.vector.tensor_scalar_mul(h[b][:, 0:P], acc[:], 0.0625)
                    nc.scalar.activation(pages[b][:].indirect(n1_list[:, 0:8]), h[b][:, 0:P], COPY)
                quantize_z(1, 0, P)
            for b in blocks:
                page = pages[b]
                fetched = sb.tile([P, S], F32, name=f"fetched{b}")
                if pair == 0:
                    acc = psum.tile([P, P], F32, name=f"acc{b}")
                    second_product(acc[:], b, d_picked, 1)
                    nc.vector.tensor_scalar_mul(h[b][:, P:S], acc[:], 0.0625)
                    nc.scalar.activation(fetched[:], h[b][:].indirect(n3_list[:]), COPY)
                    nc.scalar.activation(page[:].indirect(n1_list[:, 8:16]), h[b][:, P:S], COPY)
                else:
                    acc = psum.tile([P, S], F32, name=f"acc{b}")
                    for u in range(2):
                        second_product(acc[:, u * P : (u + 1) * P], b, d_picked, u)
                    nc.vector.tensor_scalar_mul(h[b][:, 0:S], acc[:], 0.0625)
                    nc.scalar.activation(fetched[:], h[b][:].indirect(n3_list[:]), COPY)
                    nc.scalar.activation(page[:].indirect(n1_list[:]), h[b][:, 0:S], COPY)
                nw = sb.tile([P, S], F32, name=f"nw{b}")
                nc.vector.tensor_tensor(nw[:], h[b][:, 0:S], fetched[:], SUBTRACT)
                nc.scalar.activation(page[:].indirect(n2_list[:]), nw[:], COPY)
                (nc.sync if b >= 2 else nc.gpsimd).dma_start(out[b * P : (b + 1) * P, :], page[:])
